import numpy as np
import ml_dtypes

BF16 = ml_dtypes.bfloat16


def bf(x):
    return np.asarray(x, np.float32).astype(BF16)


def f32(x):
    return np.asarray(x, np.float32)


def f64(x):
    return np.asarray(x).astype(np.float64)


def striped(idx):
    return np.tile(idx.reshape(-1, 16).T, (8, 1))


S, A, K, M, N, E, Q = 256, 256, 256, 512, 128, 2, 64


def setup_inputs():
    return {"x": bf(np.random.standard_normal((A, S))), "wd": bf(np.random.standard_normal((A, M)) / np.sqrt(A)), "y": bf(np.random.standard_normal((K, N))), "w": bf(np.random.standard_normal((E, K, M)) / np.sqrt(K)), "b": f32(0.5 * np.random.standard_normal((M, 1))), "offs": striped(np.random.permutation(S)[:N])}


def reference(x, wd, y, w, b, offs):
    idx = offs[:16].T.reshape(-1)
    z = f64(wd).T @ f64(x)
    for e in range(E):
        z[:, idx[e * Q : (e + 1) * Q]] += f64(w)[e].T @ f64(y)[:, e * Q : (e + 1) * Q]
    return np.tanh(z + f64(b))

@@ -1,0 +1,62 @@
+import concourse.mybir as mybir
+
+BF16, F32, U16 = mybir.dt.bfloat16, mybir.dt.float32, mybir.dt.uint16
+TANH = mybir.ActivationFunctionType.Tanh
+
+P = 128
+TOKENS, DENSE_IN, EXPERT_IN, FEATURES, ENTRIES, EXPERTS = 256, 256, 256, 512, 128, 2
+PIECE = ENTRIES // EXPERTS
+FLOPS = 2 * DENSE_IN * FEATURES * TOKENS + 2 * EXPERT_IN * FEATURES * ENTRIES
+
+
+def tile_rows_fillproj_tanh_kernel(tc, x, wd, y, w, b, offs, out):
+    nc = tc.nc
+    blocks_in = DENSE_IN // P
+    windows_out = FEATURES // P
+
+    with (
+        tc.tile_pool(name="held", bufs=1) as held,
+        tc.psum_pool(name="windows", bufs=1) as windows,
+    ):
+        offsets = held.tile([P, ENTRIES // 16], U16)
+        x_tile = held.tile([P, blocks_in * TOKENS], BF16)
+        wd_tile = held.tile([P, blocks_in * FEATURES], BF16)
+        y_tile = held.tile([P, blocks_in * ENTRIES], BF16)
+        w_tiles = [held.tile([P, blocks_in * FEATURES], BF16, name=f"w_tile{e}") for e in range(EXPERTS)]
+        bias = held.tile([P, windows_out], F32)
+
+        nc.sync.dma_start(x_tile[:], x.rearrange("(p a) s -> p (a s)", a=blocks_in))
+        nc.sync.dma_start(wd_tile[:], wd.rearrange("(p a) m -> p (a m)", a=blocks_in))
+        nc.sync.dma_start(offsets[:], offs)
+        nc.sync.dma_start(y_tile[:], y.rearrange("(p a) j -> p (a j)", a=blocks_in))
+        for e in range(EXPERTS):
+            nc.sync.dma_start(w_tiles[e][:], w[e].rearrange("(p a) m -> p (a m)", a=blocks_in))
+        nc.sync.dma_start(bias[:], b.rearrange("(i p) o -> p (i o)", p=P))
+
+        zs = [windows.tile([P, TOKENS], F32, name=f"z{i}") for i in range(windows_out)]
+        for i in range(windows_out):
+            for a in range(blocks_in):
+                nc.tensor.matmul(
+                    zs[i][:],
+                    wd_tile[:, a * FEATURES + i * P : a * FEATURES + (i + 1) * P],
+                    x_tile[:, a * TOKENS : (a + 1) * TOKENS],
+                    start=(a == 0),
+                    stop=False,
+                )
+
+        for i in range(windows_out):
+            for e in range(EXPERTS):
+                piece = offsets[:, e * PIECE // 16 : (e + 1) * PIECE // 16]
+                for a in range(blocks_in):
+                    nc.tensor.matmul(
+                        zs[i][:].indirect(piece),
+                        w_tiles[e][:, a * FEATURES + i * P : a * FEATURES + (i + 1) * P],
+                        y_tile[:, a * ENTRIES + e * PIECE : a * ENTRIES + (e + 1) * PIECE],
+                        start=False,
+                        stop=(e == EXPERTS - 1 and a == blocks_in - 1),
+                    )
+
+        for i in range(windows_out):
+            result = held.tile([P, TOKENS], F32, name=f"result{i}")
+            nc.scalar.activation(result[:], zs[i][:], TANH, bias=bias[:, i : i + 1])
+            nc.sync.dma_start(out[i * P : (i + 1) * P, :], result[:])

@@ -6,6 +6,7 @@ TANH = mybir.ActivationFunctionType.Tanh
 P = 128
 TOKENS, DENSE_IN, EXPERT_IN, FEATURES, ENTRIES, EXPERTS = 256, 256, 256, 512, 128, 2
 PIECE = ENTRIES // EXPERTS
+WARM_UPS = 8
 FLOPS = 2 * DENSE_IN * FEATURES * TOKENS + 2 * EXPERT_IN * FEATURES * ENTRIES
 
 
@@ -18,6 +19,14 @@ def tile_rows_fillproj_tanh_kernel(tc, x, wd, y, w, b, offs, out):
         tc.tile_pool(name="held", bufs=1) as held,
         tc.psum_pool(name="windows", bufs=1) as windows,
     ):
+        zeros = held.tile([P, TOKENS], BF16)
+        nc.vector.memset(zeros[:], 0.0)
+        warm_bank = windows.tile([P, TOKENS], F32)
+        for step in range(WARM_UPS):
+            nc.tensor.matmul(warm_bank[:], zeros[:, :P], zeros[:], start=True, stop=True)
+        warm_tanh = held.tile([P, 1], BF16)
+        nc.scalar.activation(warm_tanh[:], zeros[:, 0:1], TANH)
+
         offsets = held.tile([P, ENTRIES // 16], U16)
         x_tile = held.tile([P, blocks_in * TOKENS], BF16)
         wd_tile = held.tile([P, blocks_in * FEATURES], BF16)
@@ -44,9 +53,9 @@ def tile_rows_fillproj_tanh_kernel(tc, x, wd, y, w, b, offs, out):
                     stop=False,
                 )
 
-        for i in range(windows_out):
-            for e in range(EXPERTS):
-                piece = offsets[:, e * PIECE // 16 : (e + 1) * PIECE // 16]
+        for e in range(EXPERTS):
+            piece = offsets[:, e * PIECE // 16 : (e + 1) * PIECE // 16]
+            for i in range(windows_out):
                 for a in range(blocks_in):
                     nc.tensor.matmul(
                         zs[i][:].indirect(piece),

@@ -6,14 +6,15 @@ TANH = mybir.ActivationFunctionType.Tanh
 P = 128
 TOKENS, DENSE_IN, EXPERT_IN, FEATURES, ENTRIES, EXPERTS = 256, 256, 256, 512, 128, 2
 PIECE = ENTRIES // EXPERTS
-WARM_UPS = 8
+DENSE_BLOCKS, EXPERT_BLOCKS = DENSE_IN // P, EXPERT_IN // P
+HALVES = 2
+HALF = FEATURES // HALVES
+WARM_UPS = 6
 FLOPS = 2 * DENSE_IN * FEATURES * TOKENS + 2 * EXPERT_IN * FEATURES * ENTRIES
 
 
 def tile_rows_fillproj_tanh_kernel(tc, x, wd, y, w, b, offs, out):
     nc = tc.nc
-    blocks_in = DENSE_IN // P
-    windows_out = FEATURES // P
 
     with (
         tc.tile_pool(name="held", bufs=1) as held,
@@ -28,44 +29,44 @@ def tile_rows_fillproj_tanh_kernel(tc, x, wd, y, w, b, offs, out):
         nc.scalar.activation(warm_tanh[:], zeros[:, 0:1], TANH)
 
         offsets = held.tile([P, ENTRIES // 16], U16)
-        x_tile = held.tile([P, blocks_in * TOKENS], BF16)
-        wd_tile = held.tile([P, blocks_in * FEATURES], BF16)
-        y_tile = held.tile([P, blocks_in * ENTRIES], BF16)
-        w_tiles = [held.tile([P, blocks_in * FEATURES], BF16, name=f"w_tile{e}") for e in range(EXPERTS)]
-        bias = held.tile([P, windows_out], F32)
+        x_tile = held.tile([P, DENSE_BLOCKS, TOKENS], BF16)
+        y_tile = held.tile([P, EXPERT_BLOCKS, ENTRIES], BF16)
+        wd_halves = [held.tile([P, DENSE_BLOCKS, HALF], BF16, name=f"wd_half{h}") for h in range(HALVES)]
+        w_halves = [held.tile([P, EXPERTS * EXPERT_BLOCKS, HALF], BF16, name=f"w_half{h}") for h in range(HALVES)]
+        bias = held.tile([P, HALVES, 2], F32)
 
-        nc.sync.dma_start(x_tile[:], x.rearrange("(p a) s -> p (a s)", a=blocks_in))
-        nc.sync.dma_start(wd_tile[:], wd.rearrange("(p a) m -> p (a m)", a=blocks_in))
+        wd_rows = wd.rearrange("(p a) m -> p a m", a=DENSE_BLOCKS)
+        w_rows = w.rearrange("e (a p) m -> p (e a) m", p=P)
+        nc.sync.dma_start(x_tile[:], x.rearrange("(p a) s -> p a s", a=DENSE_BLOCKS))
+        nc.sync.dma_start(wd_halves[0][:], wd_rows[:, :, :HALF])
+        nc.sync.dma_start(wd_halves[1][:], wd_rows[:, :, HALF:])
         nc.sync.dma_start(offsets[:], offs)
-        nc.sync.dma_start(y_tile[:], y.rearrange("(p a) j -> p (a j)", a=blocks_in))
-        for e in range(EXPERTS):
-            nc.sync.dma_start(w_tiles[e][:], w[e].rearrange("(p a) m -> p (a m)", a=blocks_in))
-        nc.sync.dma_start(bias[:], b.rearrange("(i p) o -> p (i o)", p=P))
+        nc.sync.dma_start(y_tile[:], y.rearrange("(a p) j -> p a j", p=P))
+        nc.sync.dma_start(w_halves[0][:], w_rows[:, :, :HALF])
+        nc.sync.dma_start(bias[:], b.rearrange("(h p i) o -> p h (i o)", h=HALVES, i=2))
+        nc.sync.dma_start(w_halves[1][:], w_rows[:, :, HALF:])
 
-        zs = [windows.tile([P, TOKENS], F32, name=f"z{i}") for i in range(windows_out)]
-        for i in range(windows_out):
-            for a in range(blocks_in):
-                nc.tensor.matmul(
-                    zs[i][:],
-                    wd_tile[:, a * FEATURES + i * P : a * FEATURES + (i + 1) * P],
-                    x_tile[:, a * TOKENS : (a + 1) * TOKENS],
-                    start=(a == 0),
-                    stop=False,
-                )
+        zs = [windows.tile([P, TOKENS], F32, name=f"z{n}") for n in range(2 * HALVES)]
 
-        for e in range(EXPERTS):
-            piece = offsets[:, e * PIECE // 16 : (e + 1) * PIECE // 16]
-            for i in range(windows_out):
-                for a in range(blocks_in):
+        for n, z in enumerate(zs):
+            for a in range(DENSE_BLOCKS):
+                weights = wd_halves[n // 2][:, a, n % 2 :: 2]
+                nc.tensor.matmul(z[:], weights, x_tile[:, a, :], start=(a == 0), stop=False)
+
+        for n, z in enumerate(zs):
+            for e in range(EXPERTS):
+                piece = offsets[:, e * PIECE // 16 : (e + 1) * PIECE // 16]
+                for a in range(EXPERT_BLOCKS):
                     nc.tensor.matmul(
-                        zs[i][:].indirect(piece),
-                        w_tiles[e][:, a * FEATURES + i * P : a * FEATURES + (i + 1) * P],
-                        y_tile[:, a * ENTRIES + e * PIECE : a * ENTRIES + (e + 1) * PIECE],
+                        z[:].indirect(piece),
+                        w_halves[n // 2][:, e * EXPERT_BLOCKS + a, n % 2 :: 2],
+                        y_tile[:, a, e * PIECE : (e + 1) * PIECE],
                         start=False,
-                        stop=(e == EXPERTS - 1 and a == blocks_in - 1),
+                        stop=(e == EXPERTS - 1 and a == EXPERT_BLOCKS - 1),
                     )
 
-        for i in range(windows_out):
-            result = held.tile([P, TOKENS], F32, name=f"result{i}")
-            nc.scalar.activation(result[:], zs[i][:], TANH, bias=bias[:, i : i + 1])
-            nc.sync.dma_start(out[i * P : (i + 1) * P, :], result[:])
+        out_rows = out.rearrange("(h p i) s -> h i p s", h=HALVES, i=2)
+        for n, z in enumerate(zs):
+            result = held.tile([P, TOKENS], F32, name=f"result{n}")
+            nc.scalar.activation(result[:], z[:], TANH, bias=bias[:, n // 2, n % 2 : n % 2 + 1])
+            nc.sync.dma_start(out_rows[n // 2, n % 2], result[:])

import concourse.mybir as mybir

BF16, F32, U16 = mybir.dt.bfloat16, mybir.dt.float32, mybir.dt.uint16
TANH = mybir.ActivationFunctionType.Tanh

P = 128
TOKENS, DENSE_IN, EXPERT_IN, FEATURES, ENTRIES, EXPERTS = 256, 256, 256, 512, 128, 2
PIECE = ENTRIES // EXPERTS
DENSE_BLOCKS, EXPERT_BLOCKS = DENSE_IN // P, EXPERT_IN // P
HALVES = 2
HALF = FEATURES // HALVES
WARM_UPS = 6
FLOPS = 2 * DENSE_IN * FEATURES * TOKENS + 2 * EXPERT_IN * FEATURES * ENTRIES


def tile_rows_fillproj_tanh_kernel(tc, x, wd, y, w, b, offs, out):
    nc = tc.nc

    with (
        tc.tile_pool(name="held", bufs=1) as held,
        tc.psum_pool(name="windows", bufs=1) as windows,
    ):
        zeros = held.tile([P, TOKENS], BF16)
        nc.vector.memset(zeros[:], 0.0)
        warm_bank = windows.tile([P, TOKENS], F32)
        for step in range(WARM_UPS):
            nc.tensor.matmul(warm_bank[:], zeros[:, :P], zeros[:], start=True, stop=True)
        warm_tanh = held.tile([P, 1], BF16)
        nc.scalar.activation(warm_tanh[:], zeros[:, 0:1], TANH)

        offsets = held.tile([P, ENTRIES // 16], U16)
        x_tile = held.tile([P, DENSE_BLOCKS, TOKENS], BF16)
        y_tile = held.tile([P, EXPERT_BLOCKS, ENTRIES], BF16)
        wd_halves = [held.tile([P, DENSE_BLOCKS, HALF], BF16, name=f"wd_half{h}") for h in range(HALVES)]
        w_halves = [held.tile([P, EXPERTS * EXPERT_BLOCKS, HALF], BF16, name=f"w_half{h}") for h in range(HALVES)]
        bias = held.tile([P, HALVES, 2], F32)

        wd_rows = wd.rearrange("(p a) m -> p a m", a=DENSE_BLOCKS)
        w_rows = w.rearrange("e (a p) m -> p (e a) m", p=P)
        nc.sync.dma_start(x_tile[:], x.rearrange("(p a) s -> p a s", a=DENSE_BLOCKS))
        nc.sync.dma_start(wd_halves[0][:], wd_rows[:, :, :HALF])
        nc.sync.dma_start(wd_halves[1][:], wd_rows[:, :, HALF:])
        nc.sync.dma_start(offsets[:], offs)
        nc.sync.dma_start(y_tile[:], y.rearrange("(a p) j -> p a j", p=P))
        nc.sync.dma_start(w_halves[0][:], w_rows[:, :, :HALF])
        nc.sync.dma_start(bias[:], b.rearrange("(h p i) o -> p h (i o)", h=HALVES, i=2))
        nc.sync.dma_start(w_halves[1][:], w_rows[:, :, HALF:])

        zs = [windows.tile([P, TOKENS], F32, name=f"z{n}") for n in range(2 * HALVES)]

        for n, z in enumerate(zs):
            for a in range(DENSE_BLOCKS):
                weights = wd_halves[n // 2][:, a, n % 2 :: 2]
                nc.tensor.matmul(z[:], weights, x_tile[:, a, :], start=(a == 0), stop=False)

        for n, z in enumerate(zs):
            for e in range(EXPERTS):
                piece = offsets[:, e * PIECE // 16 : (e + 1) * PIECE // 16]
                for a in range(EXPERT_BLOCKS):
                    nc.tensor.matmul(
                        z[:].indirect(piece),
                        w_halves[n // 2][:, e * EXPERT_BLOCKS + a, n % 2 :: 2],
                        y_tile[:, a, e * PIECE : (e + 1) * PIECE],
                        start=False,
                        stop=(e == EXPERTS - 1 and a == EXPERT_BLOCKS - 1),
                    )

        out_rows = out.rearrange("(h p i) s -> h i p s", h=HALVES, i=2)
        for n, z in enumerate(zs):
            result = held.tile([P, TOKENS], F32, name=f"result{n}")
            nc.scalar.activation(result[:], z[:], TANH, bias=bias[:, n // 2, n % 2 : n % 2 + 1])
            nc.sync.dma_start(out_rows[n // 2, n % 2], result[:])
